import numpy as np
import ml_dtypes


def mxq(x, axis, fmt="e4m3"):
    dtype, down = {"e4m3": (ml_dtypes.float8_e4m3fn, 7), "e5m2": (ml_dtypes.float8_e5m2, 14)}[fmt]
    v = np.moveaxis(np.asarray(x, np.float32).astype(ml_dtypes.bfloat16).astype(np.float64), axis, -1)
    blocks = v.reshape(v.shape[:-1] + (-1, 32))
    amax = np.abs(blocks).max(-1, keepdims=True)
    byte = np.maximum(np.where(amax > 0, np.frexp(amax)[1] - 1 + 127, 0) - down, 1)
    scale = np.exp2(byte - 127.0)
    codes = (blocks / scale).astype(np.float32).astype(dtype).astype(np.float64)
    return np.moveaxis((codes * scale).reshape(v.shape), -1, axis)


WIDE = False


def mx_kscale(k):
    if not WIDE:
        return np.ones(k)
    levels = np.array([30, -30])
    if k % 512:
        return np.exp2(np.random.permutation(np.resize(levels, k // 32))).repeat(32)
    a = np.empty((k // 512, 16))
    for p in range(k // 512):
        a[p, :8] = np.random.permutation(np.resize(levels, 8))
        for g in range(8):
            far = levels[np.abs(levels - a[p, g]) >= 10]
            a[p, g + 8] = far[np.random.randint(len(far))]
    return np.exp2(a.ravel()).repeat(32)


def f64(x):
    return np.asarray(x).astype(np.float64)


def striped(idx):
    return np.tile(np.asarray(idx).reshape(-1, 16).T, (8, 1)).astype(np.uint16)


def unstriped(offs):
    return offs[:16].T.reshape(-1).astype(np.int64)


E2M1 = np.array([0.0, 0.5, 1.0, 1.5, 2.0, 3.0, 4.0, 6.0, -0.0, -0.5, -1.0, -1.5, -2.0, -3.0, -4.0, -6.0])


def pack_weight(w, fmt):
    k, n = w.shape
    w = f64(np.asarray(w, np.float32).astype(ml_dtypes.bfloat16)).reshape(k // 32, 32, n)
    amax = np.abs(w).max(1)
    if fmt in ("e4m3", "e5m2"):
        byte = np.frexp(amax)[1] - 1 + 127 - (7 if fmt == "e4m3" else 14)
    else:
        mant, ex = np.frexp(amax / 6.0)
        byte = np.where(mant > 0.5, ex, ex - 1) + 127
    byte = np.clip(np.where(amax > 0, byte, 1), 1, 254)
    scaled = (w * np.exp2(127.0 - byte)[:, None, :]).reshape(k, n).astype(np.float32)
    by_word = np.ascontiguousarray(scaled.reshape(k // 512, 128, 4, n).transpose(0, 1, 3, 2))
    if fmt in ("e4m3", "e5m2"):
        words = by_word.astype(ml_dtypes.float8_e4m3fn if fmt == "e4m3" else ml_dtypes.float8_e5m2).view(np.uint8)
    else:
        c = by_word.astype(ml_dtypes.float4_e2m1fn).view(np.uint8) & 0xF
        words = (c[..., 0::2] | (c[..., 1::2] << 4)).reshape(k // 512, 128, 2 * n)
    return np.ascontiguousarray(words), np.ascontiguousarray(byte.astype(np.uint8).reshape(k // 512, 16, n))


def unpack_weight(words, scales, fmt):
    g, _, n = scales.shape
    words = np.ascontiguousarray(words).reshape(g, 128, n, -1)
    if fmt in ("e4m3", "e5m2"):
        vals = words.view(ml_dtypes.float8_e4m3fn if fmt == "e4m3" else ml_dtypes.float8_e5m2).astype(np.float64)
    else:
        nib = np.empty((g, 128, n, 4), np.uint8)
        nib[..., 0::2] = words & 0xF
        nib[..., 1::2] = words >> 4
        vals = E2M1[nib]
    vals = vals * np.repeat(np.exp2(scales.astype(np.float64) - 127.0), 8, axis=1)[..., None]
    return vals.transpose(0, 1, 3, 2).reshape(g * 512, n)


def sigmoid(v):
    return 1.0 / (1.0 + np.exp(-v))


def sgn(shape):
    return np.random.uniform(0.5, 2.0, shape) * np.where(np.random.standard_normal(shape) < 0, -1.0, 1.0)


K, T, J, R, O, N, S, E = 512, 1024, 256, 512, 128, 256, 1024, 1024


def setup_inputs():
    n = np.random.standard_normal
    idx = np.random.permutation(T)[:J]
    idx2 = np.random.permutation(J)[:O]
    idx3 = np.random.permutation(J)[:O]
    idx4 = np.random.permutation(S)[:N]
    idx5 = np.random.permutation(E)[:O]
    fk = mx_kscale(K)
    fr = mx_kscale(R)
    xtp = pack_weight(n((K, T)) / fk[:, None], "e5m2")
    wp = pack_weight(n((K, R)) * 1 / np.sqrt(K) * fk[:, None], "e2m1")
    vsp = pack_weight(n((R, S)) * 1 / np.sqrt(R) / fr[:, None], "e2m1")
    return {
        "xt_words": xtp[0],
        "xt_scales": xtp[1],
        "w_words": wp[0],
        "w_scales": wp[1],
        "sa": (np.random.uniform(0.5, 1.6, (R, 1)) * fr[:, None]).astype(np.float32),
        "sg": (sgn((R, 1))).astype(np.float32),
        "bg": (np.random.uniform(-2.0, 2.0, (R, 1))).astype(np.float32),
        "vs_words": vsp[0],
        "vs_scales": vsp[1],
        "offs": striped(idx),
        "offs2": striped(idx2),
        "offs3": striped(idx3),
        "offs4": striped(idx4),
        "offs5": striped(idx5),
    }


def reference(xt_words, xt_scales, w_words, w_scales, sa, sg, bg, vs_words, vs_scales, offs, offs2, offs3, offs4, offs5):
    idx = unstriped(offs)
    idx2 = unstriped(offs2)
    idx3 = unstriped(offs3)
    idx4 = unstriped(offs4)
    idx5 = unstriped(offs5)
    xtu = unpack_weight(xt_words, xt_scales, "e5m2")
    wu = unpack_weight(w_words, w_scales, "e2m1")
    vsu = unpack_weight(vs_words, vs_scales, "e2m1")
    xtidxg = xtu[:, idx]
    a = wu.T @ xtidxg
    hid = a[:, idx2] * f64(sa) * sigmoid(a[:, idx3] * f64(sg) + f64(bg))
    vsidx4g = vsu[:, idx4]
    hidq = mxq(hid, 0, "e4m3")
    p = vsidx4g.T @ hidq
    y = np.zeros((N, E))
    y[:, idx5] = p
    return y

@@ -1,0 +1,145 @@
+from contextlib import ExitStack
+
+import concourse.mybir as mybir
+
+F32 = mybir.dt.float32
+BF16 = mybir.dt.bfloat16
+I32 = mybir.dt.int32
+U32 = mybir.dt.uint32
+U16 = mybir.dt.uint16
+U8 = mybir.dt.uint8
+E4M3X4 = mybir.dt.float8_e4m3fn_x4
+E5M2X4 = mybir.dt.float8_e5m2_x4
+E2M1X4 = mybir.dt.float4_e2m1fn_x4
+ACT = mybir.ActivationFunctionType
+MULT = mybir.AluOpType.mult
+
+P = 128
+PACK = 4
+K, T, J, R, O, N, S, E = 512, 1024, 256, 512, 128, 256, 1024, 1024
+FLOPS = 2 * K * R * J + 2 * R * N * O
+
+
+def tile_list_gatedpick_solo_store_scattered_kernel(
+    tc, xt_words, xt_scales, w_words, w_scales, sa, sg, bg, vs_words, vs_scales,
+    offs, offs2, offs3, offs4, offs5, out,
+):
+    nc = tc.nc
+    with ExitStack() as ctx:
+        lists = ctx.enter_context(tc.tile_pool(name="lists", bufs=1))
+        sb = ctx.enter_context(tc.tile_pool(name="sb", bufs=1))
+        ps = ctx.enter_context(tc.psum_pool(name="ps", bufs=1))
+
+        l1 = lists.tile([P, J // 16], U16, name="l1")
+        l2 = lists.tile([P, O // 16], U16, name="l2")
+        l3 = lists.tile([P, O // 16], U16, name="l3")
+        l4 = lists.tile([P, N // 16], U16, name="l4")
+        l5 = lists.tile([P, O // 16], U16, name="l5")
+
+        xw = sb.tile([P, T], I32, name="xw", align_bytes=64)
+        xs = sb.tile([P, T], U8, name="xs", align_bytes=64)
+        ww = sb.tile([P, R], U16, name="ww", align_bytes=64)
+        ws_stage = sb.tile([PACK, 4, R // 4], I32, name="ws_stage", align_bytes=64)
+        ws = sb.tile([P, R], U8, name="ws", align_bytes=64)
+        vw = sb.tile([P, S], U16, name="vw", align_bytes=64)
+        vsc = sb.tile([P, S], U8, name="vsc", align_bytes=64)
+        sa_t = sb.tile([P, PACK], F32, name="sa_t")
+        sg_t = sb.tile([P, PACK], F32, name="sg_t")
+        bg_t = sb.tile([P, PACK], F32, name="bg_t")
+        pages = [sb.tile([P, E], F32, name="page%d" % h, align_bytes=64) for h in range(N // P)]
+
+        nc.vector.memset(xs[:].bitcast(I32), 0)
+        nc.vector.memset(ws[:].bitcast(I32), 0)
+        nc.vector.memset(vsc[:].bitcast(I32), 0)
+
+        nc.sync.dma_start(ws_stage[:], w_scales[0].bitcast(I32).rearrange("(q r) c -> r q c", r=4))
+        nc.sync.dma_start(l1[:], offs)
+        nc.sync.dma_start(xw[:], xt_words[0].rearrange("p c i -> p (c i)").bitcast(I32))
+        nc.sync.dma_start(ww[:].bitcast(I32), w_words[0].bitcast(I32))
+        for q in range(4):
+            nc.scalar.dma_start(xs[32 * q : 32 * q + 4, :].bitcast(I32), xt_scales[0, 4 * q : 4 * q + 4, :].bitcast(I32))
+        nc.sync.dma_start(l3[:], offs3)
+        for tile, vec in ((sg_t, sg), (bg_t, bg), (sa_t, sa)):
+            nc.sync.dma_start(tile[:], vec.rearrange("(p t) one -> p (t one)", t=PACK))
+        nc.sync.dma_start(l2[:], offs2)
+        nc.sync.dma_start(l4[:], offs4)
+        nc.sync.dma_start(vw[:].bitcast(I32), vs_words[0].bitcast(I32))
+        for q in range(4):
+            nc.sync.dma_start(vsc[32 * q : 32 * q + 4, :].bitcast(I32), vs_scales[0, 4 * q : 4 * q + 4, :].bitcast(I32))
+        nc.sync.dma_start(l5[:], offs5)
+
+        for page in pages:
+            nc.vector.memset(page[:], 0.0)
+
+        for q in range(4):
+            nc.vector.tensor_copy(ws[32 * q : 32 * q + 4, :].bitcast(I32), ws_stage[:, q, :])
+        wsp = sb.tile([P, PACK, P], U8, name="wsp", align_bytes=64)
+        nc.vector.tensor_copy(wsp[:], ws[:].rearrange("p (m t) -> p t m", t=PACK))
+
+        xsg = sb.tile([P, J], U8, name="xsg", align_bytes=64)
+        nc.vector.tensor_copy(xsg[:], xs[:].indirect(l1[:]))
+        xg = sb.tile([P, J], U32, name="xg", align_bytes=64)
+        nc.vector.tensor_copy(xg[:], xw[:].bitcast(U32).indirect(l1[:]))
+
+        wwp = sb.tile([P, PACK, P], U16, name="wwp", align_bytes=64)
+        dealt = ww[:].rearrange("p (m t) -> p t m", t=PACK)
+        nc.scalar.copy(wwp[:, 0, :], dealt[:, 0, :])
+        nc.scalar.copy(wwp[:, 1:, :], dealt[:, 1:, :])
+
+        a_sb = []
+        for t in range(PACK):
+            a_ps = ps.tile([P, J], F32, name="a_ps%d" % t)
+            nc.tensor.matmul_mx(
+                out=a_ps[:], lhsT=wwp[:, t, :].bitcast(E2M1X4), lhsT_scale=wsp[:, t, :],
+                rhs=xg[:].bitcast(E5M2X4), rhs_scale=xsg[:], start=True, stop=True,
+            )
+            a_t = sb.tile([P, J], F32, name="a_sb%d" % t, align_bytes=64)
+            nc.vector.tensor_copy(a_t[:], a_ps[:])
+            a_sb.append(a_t)
+
+        vg = sb.tile([P, N], U16, name="vg", align_bytes=64)
+        nc.vector.tensor_copy(vg[:], vw[:].indirect(l4[:]))
+        vsg = sb.tile([P, N], U8, name="vsg", align_bytes=64)
+        nc.vector.tensor_copy(vsg[:], vsc[:].indirect(l4[:]))
+
+        hid = sb.tile([P, O, PACK], BF16, name="hid", align_bytes=64)
+        for u in range(2):
+            gate = sb.tile([P, 2, O], F32, name="gate%d" % u, align_bytes=64)
+            prod = sb.tile([P, 2, O], F32, name="prod%d" % u, align_bytes=64)
+            for i in range(2):
+                t = 2 * u + i
+                nc.scalar.activation(
+                    out=gate[:, i, :], in_=a_sb[t][:].indirect(l3[:]), func=ACT.Sigmoid,
+                    bias=bg_t[:, t : t + 1], scale=sg_t[:, t : t + 1],
+                )
+                nc.scalar.activation(
+                    out=prod[:, i, :], in_=a_sb[t][:].indirect(l2[:]), func=ACT.Copy,
+                    scale=sa_t[:, t : t + 1],
+                )
+            nc.vector.tensor_tensor(
+                hid[:, :, 2 * u : 2 * u + 2],
+                prod[:].rearrange("p t o -> p o t"),
+                gate[:].rearrange("p t o -> p o t"),
+                MULT,
+            )
+
+        hq = sb.tile([P, O], U32, name="hq", align_bytes=64)
+        hs = sb.tile([P, O], U8, name="hs", align_bytes=64)
+        nc.vector.quantize_mx(out=hq[:].bitcast(E4M3X4), scales=hs[:], in_=hid[:].rearrange("p o t -> p (o t)"))
+
+        for h, page in enumerate(pages):
+            cols = slice(h * P, (h + 1) * P)
+            p_ps = ps.tile([P, O], F32, name="p_ps%d" % h)
+            nc.tensor.matmul_mx(
+                out=p_ps[:], lhsT=vg[:, cols].bitcast(E2M1X4), lhsT_scale=vsg[:, cols],
+                rhs=hq[:].bitcast(E4M3X4), rhs_scale=hs[:], start=True, stop=True,
+            )
+            p_sb = sb.tile([P, O], F32, name="p_sb%d" % h, align_bytes=64)
+            if h == 0:
+                nc.vector.tensor_copy(p_sb[:], p_ps[:])
+                nc.vector.tensor_copy(page[:].indirect(l5[:]), p_sb[:])
+                nc.sync.dma_start(out[cols, :], page[:])
+            else:
+                nc.scalar.copy(p_sb[:], p_ps[:])
+                nc.scalar.activation(out=page[:].indirect(l5[:]), in_=p_sb[:], func=ACT.Copy)
+                nc.scalar.dma_start(out[cols, :], page[:])

@@ -36,28 +36,34 @@ def tile_list_gatedpick_solo_store_scattered_kernel(
         l4 = lists.tile([P, N // 16], U16, name="l4")
         l5 = lists.tile([P, O // 16], U16, name="l5")
 
-        xw = sb.tile([P, T], I32, name="xw", align_bytes=64)
+        xw = sb.tile([P, T], I32, name="xw", tag="xw_page", align_bytes=64)
         xs = sb.tile([P, T], U8, name="xs", align_bytes=64)
         ww = sb.tile([P, R], U16, name="ww", align_bytes=64)
-        ws_stage = sb.tile([PACK, 4, R // 4], I32, name="ws_stage", align_bytes=64)
-        ws = sb.tile([P, R], U8, name="ws", align_bytes=64)
+        ws = sb.tile([P, 2, R], U8, name="ws", align_bytes=64)
         vw = sb.tile([P, S], U16, name="vw", align_bytes=64)
-        vsc = sb.tile([P, S], U8, name="vsc", align_bytes=64)
+        vsc = sb.tile([P, S], U8, name="vsc", tag="vsc_hid", align_bytes=64)
         sa_t = sb.tile([P, PACK], F32, name="sa_t")
         sg_t = sb.tile([P, PACK], F32, name="sg_t")
         bg_t = sb.tile([P, PACK], F32, name="bg_t")
-        pages = [sb.tile([P, E], F32, name="page%d" % h, align_bytes=64) for h in range(N // P)]
+        page0 = sb.tile([P, E], F32, name="page0", align_bytes=64)
 
+        nc.vector.memset(ws[:].rearrange("p u c -> p (u c)").bitcast(I32), 0)
         nc.vector.memset(xs[:].bitcast(I32), 0)
-        nc.vector.memset(ws[:].bitcast(I32), 0)
+        warm_in = sb.tile([P, 1], F32, name="warm_in")
+        warm_out = sb.tile([P, 1], F32, name="warm_out")
+        nc.vector.memset(warm_in[:], 0.0)
         nc.vector.memset(vsc[:].bitcast(I32), 0)
 
-        nc.sync.dma_start(ws_stage[:], w_scales[0].bitcast(I32).rearrange("(q r) c -> r q c", r=4))
         nc.sync.dma_start(l1[:], offs)
+        ws_rows = w_scales[0].bitcast(I32).rearrange("(u q r) c -> q r u c", u=2, q=2)
+        for q in range(2):
+            nc.sync.dma_start(ws[32 * q : 32 * q + 4, :, :].bitcast(I32), ws_rows[q])
+        for q in range(4):
+            queue = nc.sync if q < 2 else nc.scalar
+            queue.dma_start(xs[32 * q : 32 * q + 4, :].bitcast(I32), xt_scales[0, 4 * q : 4 * q + 4, :].bitcast(I32))
+        nc.scalar.activation(out=warm_out[:], in_=warm_in[:], func=ACT.Sigmoid)
         nc.sync.dma_start(xw[:], xt_words[0].rearrange("p c i -> p (c i)").bitcast(I32))
         nc.sync.dma_start(ww[:].bitcast(I32), w_words[0].bitcast(I32))
-        for q in range(4):
-            nc.scalar.dma_start(xs[32 * q : 32 * q + 4, :].bitcast(I32), xt_scales[0, 4 * q : 4 * q + 4, :].bitcast(I32))
         nc.sync.dma_start(l3[:], offs3)
         for tile, vec in ((sg_t, sg), (bg_t, bg), (sa_t, sa)):
             nc.sync.dma_start(tile[:], vec.rearrange("(p t) one -> p (t one)", t=PACK))
@@ -68,41 +74,53 @@ def tile_list_gatedpick_solo_store_scattered_kernel(
             nc.sync.dma_start(vsc[32 * q : 32 * q + 4, :].bitcast(I32), vs_scales[0, 4 * q : 4 * q + 4, :].bitcast(I32))
         nc.sync.dma_start(l5[:], offs5)
 
-        for page in pages:
-            nc.vector.memset(page[:], 0.0)
+        nc.vector.memset(page0[:], 0.0)
 
-        for q in range(4):
-            nc.vector.tensor_copy(ws[32 * q : 32 * q + 4, :].bitcast(I32), ws_stage[:, q, :])
+        nc.vector.tensor_copy(ws[64:128, 0, :].bitcast(I32), ws[0:64, 1, :].bitcast(I32))
         wsp = sb.tile([P, PACK, P], U8, name="wsp", align_bytes=64)
-        nc.vector.tensor_copy(wsp[:], ws[:].rearrange("p (m t) -> p t m", t=PACK))
+        nc.vector.tensor_copy(wsp[:], ws[:, 0, :].rearrange("p (m t) -> p t m", t=PACK))
 
         xsg = sb.tile([P, J], U8, name="xsg", align_bytes=64)
         nc.vector.tensor_copy(xsg[:], xs[:].indirect(l1[:]))
         xg = sb.tile([P, J], U32, name="xg", align_bytes=64)
-        nc.vector.tensor_copy(xg[:], xw[:].bitcast(U32).indirect(l1[:]))
+        for u in range(2):
+            nc.vector.tensor_copy(xg[:, u * P : (u + 1) * P], xw[:].bitcast(U32).indirect(l1[:, 8 * u : 8 * u + 8]))
+        page1 = sb.tile([P, E], F32, name="page1", tag="xw_page", align_bytes=64)
+        nc.gpsimd.memset(page1[:], 0.0)
+        pages = [page0, page1]
 
         wwp = sb.tile([P, PACK, P], U16, name="wwp", align_bytes=64)
         dealt = ww[:].rearrange("p (m t) -> p t m", t=PACK)
         nc.scalar.copy(wwp[:, 0, :], dealt[:, 0, :])
-        nc.scalar.copy(wwp[:, 1:, :], dealt[:, 1:, :])
+        nc.scalar.copy(wwp[:, 1, :], dealt[:, 1, :])
+        nc.scalar.copy(wwp[:, 2:, :], dealt[:, 2:, :])
 
-        a_sb = []
-        for t in range(PACK):
+        a_sb = [sb.tile([P, J], F32, name="a_sb%d" % t, align_bytes=64) for t in range(PACK)]
+        for u in range(2):
+            cols = slice(u * P, (u + 1) * P)
+            a_half = ps.tile([P, P], F32, name="a_half%d" % u)
+            nc.tensor.matmul_mx(
+                out=a_half[:], lhsT=wwp[:, 0, :].bitcast(E2M1X4), lhsT_scale=wsp[:, 0, :],
+                rhs=xg[:, cols].bitcast(E5M2X4), rhs_scale=xsg[:, cols], start=True, stop=True,
+            )
+            if u == 0:
+                nc.scalar.copy(a_sb[0][:, cols], a_half[:])
+            else:
+                nc.vector.tensor_copy(a_sb[0][:, cols], a_half[:])
+        for t in range(1, PACK):
             a_ps = ps.tile([P, J], F32, name="a_ps%d" % t)
             nc.tensor.matmul_mx(
                 out=a_ps[:], lhsT=wwp[:, t, :].bitcast(E2M1X4), lhsT_scale=wsp[:, t, :],
                 rhs=xg[:].bitcast(E5M2X4), rhs_scale=xsg[:], start=True, stop=True,
             )
-            a_t = sb.tile([P, J], F32, name="a_sb%d" % t, align_bytes=64)
-            nc.vector.tensor_copy(a_t[:], a_ps[:])
-            a_sb.append(a_t)
+            nc.vector.tensor_copy(a_sb[t][:], a_ps[:])
 
         vg = sb.tile([P, N], U16, name="vg", align_bytes=64)
         nc.vector.tensor_copy(vg[:], vw[:].indirect(l4[:]))
         vsg = sb.tile([P, N], U8, name="vsg", align_bytes=64)
         nc.vector.tensor_copy(vsg[:], vsc[:].indirect(l4[:]))
 
-        hid = sb.tile([P, O, PACK], BF16, name="hid", align_bytes=64)
+        hid = sb.tile([P, O, PACK], BF16, name="hid", tag="vsc_hid", align_bytes=64)
         for u in range(2):
             gate = sb.tile([P, 2, O], F32, name="gate%d" % u, align_bytes=64)
             prod = sb.tile([P, 2, O], F32, name="prod%d" % u, align_bytes=64)

from contextlib import ExitStack

import concourse.mybir as mybir

F32 = mybir.dt.float32
BF16 = mybir.dt.bfloat16
I32 = mybir.dt.int32
U32 = mybir.dt.uint32
U16 = mybir.dt.uint16
U8 = mybir.dt.uint8
E4M3X4 = mybir.dt.float8_e4m3fn_x4
E5M2X4 = mybir.dt.float8_e5m2_x4
E2M1X4 = mybir.dt.float4_e2m1fn_x4
ACT = mybir.ActivationFunctionType
MULT = mybir.AluOpType.mult

P = 128
PACK = 4
K, T, J, R, O, N, S, E = 512, 1024, 256, 512, 128, 256, 1024, 1024
FLOPS = 2 * K * R * J + 2 * R * N * O


def tile_list_gatedpick_solo_store_scattered_kernel(
    tc, xt_words, xt_scales, w_words, w_scales, sa, sg, bg, vs_words, vs_scales,
    offs, offs2, offs3, offs4, offs5, out,
):
    nc = tc.nc
    with ExitStack() as ctx:
        lists = ctx.enter_context(tc.tile_pool(name="lists", bufs=1))
        sb = ctx.enter_context(tc.tile_pool(name="sb", bufs=1))
        ps = ctx.enter_context(tc.psum_pool(name="ps", bufs=1))

        l1 = lists.tile([P, J // 16], U16, name="l1")
        l2 = lists.tile([P, O // 16], U16, name="l2")
        l3 = lists.tile([P, O // 16], U16, name="l3")
        l4 = lists.tile([P, N // 16], U16, name="l4")
        l5 = lists.tile([P, O // 16], U16, name="l5")

        xw = sb.tile([P, T], I32, name="xw", tag="xw_page", align_bytes=64)
        xs = sb.tile([P, T], U8, name="xs", align_bytes=64)
        ww = sb.tile([P, R], U16, name="ww", align_bytes=64)
        ws = sb.tile([P, 2, R], U8, name="ws", align_bytes=64)
        vw = sb.tile([P, S], U16, name="vw", align_bytes=64)
        vsc = sb.tile([P, S], U8, name="vsc", tag="vsc_hid", align_bytes=64)
        sa_t = sb.tile([P, PACK], F32, name="sa_t")
        sg_t = sb.tile([P, PACK], F32, name="sg_t")
        bg_t = sb.tile([P, PACK], F32, name="bg_t")
        page0 = sb.tile([P, E], F32, name="page0", align_bytes=64)

        nc.vector.memset(ws[:].rearrange("p u c -> p (u c)").bitcast(I32), 0)
        nc.vector.memset(xs[:].bitcast(I32), 0)
        warm_in = sb.tile([P, 1], F32, name="warm_in")
        warm_out = sb.tile([P, 1], F32, name="warm_out")
        nc.vector.memset(warm_in[:], 0.0)
        nc.vector.memset(vsc[:].bitcast(I32), 0)

        nc.sync.dma_start(l1[:], offs)
        ws_rows = w_scales[0].bitcast(I32).rearrange("(u q r) c -> q r u c", u=2, q=2)
        for q in range(2):
            nc.sync.dma_start(ws[32 * q : 32 * q + 4, :, :].bitcast(I32), ws_rows[q])
        for q in range(4):
            queue = nc.sync if q < 2 else nc.scalar
            queue.dma_start(xs[32 * q : 32 * q + 4, :].bitcast(I32), xt_scales[0, 4 * q : 4 * q + 4, :].bitcast(I32))
        nc.scalar.activation(out=warm_out[:], in_=warm_in[:], func=ACT.Sigmoid)
        nc.sync.dma_start(xw[:], xt_words[0].rearrange("p c i -> p (c i)").bitcast(I32))
        nc.sync.dma_start(ww[:].bitcast(I32), w_words[0].bitcast(I32))
        nc.sync.dma_start(l3[:], offs3)
        for tile, vec in ((sg_t, sg), (bg_t, bg), (sa_t, sa)):
            nc.sync.dma_start(tile[:], vec.rearrange("(p t) one -> p (t one)", t=PACK))
        nc.sync.dma_start(l2[:], offs2)
        nc.sync.dma_start(l4[:], offs4)
        nc.sync.dma_start(vw[:].bitcast(I32), vs_words[0].bitcast(I32))
        for q in range(4):
            nc.sync.dma_start(vsc[32 * q : 32 * q + 4, :].bitcast(I32), vs_scales[0, 4 * q : 4 * q + 4, :].bitcast(I32))
        nc.sync.dma_start(l5[:], offs5)

        nc.vector.memset(page0[:], 0.0)

        nc.vector.tensor_copy(ws[64:128, 0, :].bitcast(I32), ws[0:64, 1, :].bitcast(I32))
        wsp = sb.tile([P, PACK, P], U8, name="wsp", align_bytes=64)
        nc.vector.tensor_copy(wsp[:], ws[:, 0, :].rearrange("p (m t) -> p t m", t=PACK))

        xsg = sb.tile([P, J], U8, name="xsg", align_bytes=64)
        nc.vector.tensor_copy(xsg[:], xs[:].indirect(l1[:]))
        xg = sb.tile([P, J], U32, name="xg", align_bytes=64)
        for u in range(2):
            nc.vector.tensor_copy(xg[:, u * P : (u + 1) * P], xw[:].bitcast(U32).indirect(l1[:, 8 * u : 8 * u + 8]))
        page1 = sb.tile([P, E], F32, name="page1", tag="xw_page", align_bytes=64)
        nc.gpsimd.memset(page1[:], 0.0)
        pages = [page0, page1]

        wwp = sb.tile([P, PACK, P], U16, name="wwp", align_bytes=64)
        dealt = ww[:].rearrange("p (m t) -> p t m", t=PACK)
        nc.scalar.copy(wwp[:, 0, :], dealt[:, 0, :])
        nc.scalar.copy(wwp[:, 1, :], dealt[:, 1, :])
        nc.scalar.copy(wwp[:, 2:, :], dealt[:, 2:, :])

        a_sb = [sb.tile([P, J], F32, name="a_sb%d" % t, align_bytes=64) for t in range(PACK)]
        for u in range(2):
            cols = slice(u * P, (u + 1) * P)
            a_half = ps.tile([P, P], F32, name="a_half%d" % u)
            nc.tensor.matmul_mx(
                out=a_half[:], lhsT=wwp[:, 0, :].bitcast(E2M1X4), lhsT_scale=wsp[:, 0, :],
                rhs=xg[:, cols].bitcast(E5M2X4), rhs_scale=xsg[:, cols], start=True, stop=True,
            )
            if u == 0:
                nc.scalar.copy(a_sb[0][:, cols], a_half[:])
            else:
                nc.vector.tensor_copy(a_sb[0][:, cols], a_half[:])
        for t in range(1, PACK):
            a_ps = ps.tile([P, J], F32, name="a_ps%d" % t)
            nc.tensor.matmul_mx(
                out=a_ps[:], lhsT=wwp[:, t, :].bitcast(E2M1X4), lhsT_scale=wsp[:, t, :],
                rhs=xg[:].bitcast(E5M2X4), rhs_scale=xsg[:], start=True, stop=True,
            )
            nc.vector.tensor_copy(a_sb[t][:], a_ps[:])

        vg = sb.tile([P, N], U16, name="vg", align_bytes=64)
        nc.vector.tensor_copy(vg[:], vw[:].indirect(l4[:]))
        vsg = sb.tile([P, N], U8, name="vsg", align_bytes=64)
        nc.vector.tensor_copy(vsg[:], vsc[:].indirect(l4[:]))

        hid = sb.tile([P, O, PACK], BF16, name="hid", tag="vsc_hid", align_bytes=64)
        for u in range(2):
            gate = sb.tile([P, 2, O], F32, name="gate%d" % u, align_bytes=64)
            prod = sb.tile([P, 2, O], F32, name="prod%d" % u, align_bytes=64)
            for i in range(2):
                t = 2 * u + i
                nc.scalar.activation(
                    out=gate[:, i, :], in_=a_sb[t][:].indirect(l3[:]), func=ACT.Sigmoid,
                    bias=bg_t[:, t : t + 1], scale=sg_t[:, t : t + 1],
                )
                nc.scalar.activation(
                    out=prod[:, i, :], in_=a_sb[t][:].indirect(l2[:]), func=ACT.Copy,
                    scale=sa_t[:, t : t + 1],
                )
            nc.vector.tensor_tensor(
                hid[:, :, 2 * u : 2 * u + 2],
                prod[:].rearrange("p t o -> p o t"),
                gate[:].rearrange("p t o -> p o t"),
                MULT,
            )

        hq = sb.tile([P, O], U32, name="hq", align_bytes=64)
        hs = sb.tile([P, O], U8, name="hs", align_bytes=64)
        nc.vector.quantize_mx(out=hq[:].bitcast(E4M3X4), scales=hs[:], in_=hid[:].rearrange("p o t -> p (o t)"))

        for h, page in enumerate(pages):
            cols = slice(h * P, (h + 1) * P)
            p_ps = ps.tile([P, O], F32, name="p_ps%d" % h)
            nc.tensor.matmul_mx(
                out=p_ps[:], lhsT=vg[:, cols].bitcast(E2M1X4), lhsT_scale=vsg[:, cols],
                rhs=hq[:].bitcast(E4M3X4), rhs_scale=hs[:], start=True, stop=True,
            )
            p_sb = sb.tile([P, O], F32, name="p_sb%d" % h, align_bytes=64)
            if h == 0:
                nc.vector.tensor_copy(p_sb[:], p_ps[:])
                nc.vector.tensor_copy(page[:].indirect(l5[:]), p_sb[:])
                nc.sync.dma_start(out[cols, :], page[:])
            else:
                nc.scalar.copy(p_sb[:], p_ps[:])
                nc.scalar.activation(out=page[:].indirect(l5[:]), in_=p_sb[:], func=ACT.Copy)
                nc.scalar.dma_start(out[cols, :], page[:])
